import numpy as np
import ml_dtypes


def mxq(x, axis, fmt="e4m3"):
    dtype, down = {"e4m3": (ml_dtypes.float8_e4m3fn, 7), "e5m2": (ml_dtypes.float8_e5m2, 14)}[fmt]
    v = np.moveaxis(np.asarray(x, np.float32).astype(ml_dtypes.bfloat16).astype(np.float64), axis, -1)
    blocks = v.reshape(v.shape[:-1] + (-1, 32))
    amax = np.abs(blocks).max(-1, keepdims=True)
    byte = np.maximum(np.where(amax > 0, np.frexp(amax)[1] - 1 + 127, 0) - down, 1)
    scale = np.exp2(byte - 127.0)
    codes = (blocks / scale).astype(np.float32).astype(dtype).astype(np.float64)
    return np.moveaxis((codes * scale).reshape(v.shape), -1, axis)


WIDE = False


def mx_kscale(k):
    if not WIDE:
        return np.ones(k)
    levels = np.array([10, -10, 5, -5, 0])
    if k % 512:
        return np.exp2(np.random.permutation(np.resize(levels, k // 32))).repeat(32)
    a = np.empty((k // 512, 16))
    for p in range(k // 512):
        a[p, :8] = np.random.permutation(np.resize(levels, 8))
        for g in range(8):
            far = levels[np.abs(levels - a[p, g]) >= 10]
            a[p, g + 8] = far[np.random.randint(len(far))]
    return np.exp2(a.ravel()).repeat(32)


def f64(x):
    return np.asarray(x).astype(np.float64)


def striped(idx):
    return np.tile(idx.reshape(-1, 16).T, (8, 1)).astype(np.uint16)


def unstriped(offs):
    return offs[:16].T.reshape(-1).astype(np.int64)


E2M1 = np.array([0.0, 0.5, 1.0, 1.5, 2.0, 3.0, 4.0, 6.0, -0.0, -0.5, -1.0, -1.5, -2.0, -3.0, -4.0, -6.0])


def pack_weight(w, fmt):
    k, n = w.shape
    w = f64(np.asarray(w, np.float32).astype(ml_dtypes.bfloat16)).reshape(k // 32, 32, n)
    amax = np.abs(w).max(1)
    if fmt == "e4m3":
        byte = np.frexp(amax)[1] - 1 + 127 - 7
    else:
        mant, ex = np.frexp(amax / 6.0)
        byte = np.where(mant > 0.5, ex, ex - 1) + 127
    byte = np.clip(np.where(amax > 0, byte, 1), 1, 254)
    scaled = (w * np.exp2(127.0 - byte)[:, None, :]).reshape(k, n).astype(np.float32)
    by_word = np.ascontiguousarray(scaled.reshape(k // 512, 128, 4, n).transpose(0, 1, 3, 2))
    if fmt == "e4m3":
        words = by_word.astype(ml_dtypes.float8_e4m3fn).view(np.uint8)
    else:
        c = by_word.astype(ml_dtypes.float4_e2m1fn).view(np.uint8) & 0xF
        words = (c[..., 0::2] | (c[..., 1::2] << 4)).reshape(k // 512, 128, 2 * n)
    return np.ascontiguousarray(words), np.ascontiguousarray(byte.astype(np.uint8).reshape(k // 512, 16, n))


def unpack_weight(words, scales, fmt):
    g, _, n = scales.shape
    words = np.ascontiguousarray(words).reshape(g, 128, n, -1)
    if fmt == "e4m3":
        vals = words.view(ml_dtypes.float8_e4m3fn).astype(np.float64)
    else:
        nib = np.empty((g, 128, n, 4), np.uint8)
        nib[..., 0::2] = words & 0xF
        nib[..., 1::2] = words >> 4
        vals = E2M1[nib]
    vals = vals * np.repeat(np.exp2(scales.astype(np.float64) - 127.0), 8, axis=1)[..., None]
    return vals.transpose(0, 1, 3, 2).reshape(g * 512, n)


def gelu(v):
    return 0.5 * v * (1.0 + np.tanh(np.sqrt(2.0 / np.pi) * (v + 0.044715 * v**3)))


K, T, S, K2, TB, P, H, N = 1024, 4096, 1024, 1536, 2048, 512, 1024, 384


def setup_inputs():
    n = np.random.standard_normal
    s = mx_kscale(K)[:, None]
    s2 = mx_kscale(K2)[:, None]
    u = mx_kscale(H)[:, None]
    d = {}
    d["tab_words"], d["tab_scales"] = pack_weight(n((K, T)) * s, "e4m3")
    d["tab2_words"], d["tab2_scales"] = pack_weight(n((K2, TB)) * s2, "e4m3")
    d["offs"] = striped(np.random.permutation(T)[:S])
    d["offs2"] = striped(np.random.permutation(TB)[:P])
    d["pos1"] = striped(np.random.permutation(S)[:P])
    d["wa"] = (0.8 * n((K, H)) / K ** 0.5 / s * u.T).astype(np.float32)
    d["wc_words"], d["wc_scales"] = pack_weight(1.2 * n((K2, H)) / K2 ** 0.5 / s2, "e2m1")
    d["sit"] = np.exp(0.4 * n((H, S))).astype(np.float32)
    d["wgs"] = np.exp(0.3 * n((128, P))).astype(np.float32)
    d["gz"] = (np.exp(0.2 * n(H)) * u[:, 0]).astype(np.float32)
    d["wo"] = (0.8 * n((H, N)) / H ** 0.5 / u).astype(np.float32)
    return d


def reference(tab_words, tab_scales, tab2_words, tab2_scales, offs, offs2, pos1,
              wa, wc_words, wc_scales, sit, wgs, gz, wo):
    v = unpack_weight(tab_words, tab_scales, "e4m3")[:, unstriped(offs)]
    v2 = unpack_weight(tab2_words, tab2_scales, "e4m3")[:, unstriped(offs2)]
    wc = unpack_weight(wc_words, wc_scales, "e2m1")
    a = (mxq(f64(wa), 0, "e4m3").T @ v) * f64(sit)
    c = wc.T @ v2
    b = 0.5 * c * (1.0 + np.tanh(0.7978845608 * (c + 0.044715 * c ** 3))) + c
    placed = np.zeros((H, S))
    placed[:, unstriped(pos1)] = np.tile(f64(wgs), (H // 128, 1)) * b
    z = (a + f64(gz)[:, None]) * placed + a
    y = mxq(f64(wo), 0, "e4m3").T @ mxq(z, 0, "e4m3")
    return 1.0 / (1.0 + np.exp(-y))

@@ -1,0 +1,325 @@
+from contextlib import ExitStack
+
+import concourse.mybir as mybir
+from concourse.masks import make_identity
+
+K, T, S, K2, TB, NP, H, N = 1024, 4096, 1024, 1536, 2048, 512, 1024, 384
+FLOPS = 2 * (K * H * S + K2 * H * NP + H * N * S)
+
+F32 = mybir.dt.float32
+BF16 = mybir.dt.bfloat16
+I32 = mybir.dt.int32
+U32 = mybir.dt.uint32
+U16 = mybir.dt.uint16
+U8 = mybir.dt.uint8
+FP8X4 = mybir.dt.float8_e4m3fn_x4
+FP4X4 = mybir.dt.float4_e2m1fn_x4
+ACT = mybir.ActivationFunctionType
+ALU = mybir.AluOpType
+
+P = 128
+PASS = 512
+SLICES = H // P
+HALF = 512
+PAGE_OF = (0, 1, 0, 0, 0, 0, 0, 0)
+WA_COLS = 256
+QUARTER = 256
+BANKS = {"co": 2, "a": 3, "tr": 3}
+
+
+def tile_list_band_comfort_predictor_kernel(
+    tc, tab_words, tab_scales, tab2_words, tab2_scales, offs, offs2, pos1,
+    wa, wc_words, wc_scales, sit, wgs, gz, wo, out,
+):
+    nc = tc.nc
+    with ExitStack() as ctx:
+        lists = ctx.enter_context(tc.tile_pool(name="lists", bufs=1))
+        keep = ctx.enter_context(tc.tile_pool(name="keep", bufs=1))
+        work = ctx.enter_context(tc.tile_pool(name="work", bufs=2))
+        psum = ctx.enter_context(tc.psum_pool(name="psum", bufs=3))
+
+        offs_sb = lists.tile([P, S // 16], U16, name="offs_sb")
+        offs2_sb = lists.tile([P, NP // 16], U16, name="offs2_sb")
+        pos_sb = lists.tile([P, NP // 16], U16, name="pos_sb")
+
+        t2s = keep.tile([P, 3, TB], U8, name="t2s", align_bytes=64)
+        wcs = keep.tile([P, 3, H], U8, name="wcs", align_bytes=64)
+        ts = keep.tile([P, T], U8, name="ts", align_bytes=64)
+        wcw = keep.tile([P, 3, 2 * H], U8, name="wcw", align_bytes=64)
+        wgs_sb = keep.tile([P, NP], F32, name="wgs_sb")
+        ident = keep.tile([P, P], F32, name="ident")
+        gz_rows = keep.tile([P, P], F32, name="gz_rows")
+        gz_sb = keep.tile([P, SLICES], F32, name="gz_sb")
+        pages = [keep.tile([P, S], F32, name="page%d" % i) for i in range(2)]
+        v2w = [keep.tile([P, NP], U32, name="v2w%d" % a, align_bytes=64) for a in range(3)]
+        v2s = [keep.tile([P, NP], U8, name="v2s%d" % a, align_bytes=64) for a in range(3)]
+        vw = [keep.tile([P, S], U32, name="vw%d" % a, align_bytes=64) for a in range(2)]
+        vs = keep.tile([P, S], U8, name="vs", align_bytes=64)
+        tw = [keep.tile([P, T], I32, name="tw%d" % a, align_bytes=64) for a in range(2)]
+        wa_codes = [keep.tile([P, 2 * WA_COLS], U32, name="wa_codes%d" % q, align_bytes=64) for q in range(4)]
+        wa_scales = [keep.tile([P, 2 * WA_COLS], U8, name="wa_scales%d" % q, align_bytes=64) for q in range(4)]
+        wo_bf = keep.tile([P, 2 * N * 4], BF16, name="wo_bf", align_bytes=64)
+        wo_codes = keep.tile([P, 2 * N], U32, name="wo_codes", align_bytes=64)
+        wo_scales = keep.tile([P, 2 * N], U8, name="wo_scales", align_bytes=64)
+        z_codes = [[keep.tile([P, HALF], U32, name="z_codes%d%d" % (b, h), align_bytes=64) for h in range(2)] for b in range(2)]
+        z_scales = [[keep.tile([P, HALF], U8, name="z_scales%d%d" % (b, h), align_bytes=64) for h in range(2)] for b in range(2)]
+
+        nc.vector.memset(t2s[:].rearrange("p a t -> p (a t)").bitcast(I32), 0)
+        nc.vector.memset(wcs[:].rearrange("p a t -> p (a t)").bitcast(I32), 0)
+        nc.vector.memset(ts[:].bitcast(I32), 0)
+        for page in pages:
+            nc.vector.memset(page[:], 0.0)
+        nc.gpsimd.memset(gz_rows[:], 0.0)
+        make_identity(nc, ident[:])
+
+        nc.sync.dma_start(offs2_sb[:], offs2)
+        for q in range(4):
+            nc.sync.dma_start(
+                t2s[32 * q:32 * q + 4, :, :].bitcast(I32),
+                tab2_scales[:, 4 * q:4 * q + 4, :].rearrange("a r t -> r a t").bitcast(I32))
+        nc.sync.dma_start(pos_sb[:], pos1)
+        nc.sync.dma_start(offs_sb[:], offs)
+        nc.sync.dma_start(gz_rows[0:SLICES, :], gz.rearrange("(s p) -> s p", p=P))
+        t2w = []
+        for a in range(3):
+            t2w_a = work.tile([P, TB], I32, name="t2w%d" % a, tag="big", bufs=3, align_bytes=64)
+            t2w.append(t2w_a)
+            words = tab2_words[a].rearrange("p t i -> p (t i)").bitcast(I32)
+            width = TB // (4, 2, 1)[a]
+            for c0 in range(0, TB, width):
+                nc.sync.dma_start(t2w_a[:, c0:c0 + width], words[:, c0:c0 + width])
+        for q in range(4):
+            nc.sync.dma_start(
+                wcs[32 * q:32 * q + 4, :, :].bitcast(I32),
+                wc_scales[:, 4 * q:4 * q + 4, :].rearrange("a r t -> r a t").bitcast(I32))
+        for q in range(4):
+            nc.gpsimd.dma_start(
+                ts[32 * q + 4:32 * q + 12, :].bitcast(I32),
+                tab_scales[:, 4 * q:4 * q + 4, :].bitcast(I32))
+        nc.sync.dma_start(wcw[:].bitcast(I32), wc_words.rearrange("a p n -> p a n").bitcast(I32))
+        nc.sync.dma_start(wgs_sb[:], wgs)
+        for a in range(2):
+            nc.sync.dma_start(tw[a][:], tab_words[a].rearrange("p t i -> p (t i)").bitcast(I32))
+
+        gz_ps = psum.tile([P, P], F32, name="gz_ps", tag="tr")
+        nc.tensor.transpose(gz_ps[:], gz_rows[:], ident[:])
+        nc.scalar.copy(gz_sb[:], gz_ps[:, 0:SLICES])
+
+        for a in range(3):
+            nc.vector.tensor_copy(v2s[a][:], t2s[:, a, :].indirect(offs2_sb[:]))
+        for a in range(3):
+            nc.vector.tensor_copy(v2w[a][:], t2w[a][:].bitcast(U32).indirect(offs2_sb[:]))
+
+        sit_sb = {}
+        wa_raw = {}
+        wo_raw = []
+
+        def load_wa(q):
+            for a in range(2):
+                raw = work.tile([P, 4, WA_COLS], F32, name="wa_raw", tag="wa_raw", bufs=4)
+                nc.sync.dma_start(
+                    raw[:],
+                    wa[PASS * a:PASS * (a + 1), WA_COLS * q:WA_COLS * (q + 1)].rearrange("(p i) c -> p i c", i=4))
+                wa_raw[q, a] = raw
+
+        def load_sit(s):
+            tile = work.tile([P, S], F32, name="sit_sb", tag="sit", bufs=6)
+            nc.sync.dma_start(tile[:], sit[P * s:P * (s + 1), :])
+            sit_sb[s] = tile
+
+        def load_wo():
+            for b in range(2):
+                raw = work.tile([P, 4, N], F32, name="wo_raw", tag="big", bufs=3, align_bytes=64)
+                nc.sync.dma_start(raw[:], wo[PASS * b:PASS * (b + 1), :].rearrange("(p i) n -> p i n", i=4))
+                wo_raw.append(raw)
+
+        def interleave(dst, raw):
+            nc.scalar.copy(
+                dst.rearrange("p (c e i) -> p c i e", e=4, i=4),
+                raw.rearrange("p i (c e) -> p c i e", e=4))
+
+        def quantise_wa(q):
+            wa_bf = work.tile([P, 2 * WA_COLS * 4], BF16, name="wa_bf", align_bytes=64)
+            for a in range(2):
+                interleave(wa_bf[:, 4 * WA_COLS * a:4 * WA_COLS * (a + 1)], wa_raw[q, a][:])
+            nc.vector.quantize_mx(out=wa_codes[q][:].bitcast(FP8X4), scales=wa_scales[q][:], in_=wa_bf[:])
+
+        def quantise_wo():
+            for b in range(2):
+                interleave(wo_bf[:, 4 * N * b:4 * N * (b + 1)], wo_raw[b][:])
+            for c0, c1 in ((0, 512), (512, 768)):
+                nc.vector.quantize_mx(
+                    out=wo_codes[:, c0:c1].bitcast(FP8X4), scales=wo_scales[:, c0:c1], in_=wo_bf[:, 4 * c0:4 * c1])
+
+        b_of = {}
+
+        def measure(s, tag):
+            c_ps = psum.tile([P, NP], F32, name="c_ps", tag=tag, bufs=BANKS[tag])
+            for a in range(3):
+                nc.tensor.matmul_mx(
+                    out=c_ps[:],
+                    lhsT=wcw[:, a, 2 * P * s:2 * P * (s + 1)].bitcast(FP4X4),
+                    lhsT_scale=wcs[:, a, P * s:P * (s + 1)],
+                    rhs=v2w[a][:].bitcast(FP8X4), rhs_scale=v2s[a][:],
+                    start=(a == 0), stop=(a == 2))
+            b_sb = keep.tile([P, NP], F32, name="b_sb%d" % s)
+            nc.scalar.activation(b_sb[:], c_ps[:], ACT.Gelu_apprx_tanh)
+            nc.vector.tensor_tensor(b_sb[:], c_ps[:], b_sb[:], ALU.add)
+            b_of[s] = b_sb
+
+        def place(s):
+            nc.vector.tensor_tensor(pages[PAGE_OF[s]][:].indirect(pos_sb[:]), b_of[s][:], wgs_sb[:], ALU.mult)
+
+        zt = {}
+
+        a_of = {}
+
+        def frames(s, h):
+            q, c0 = divmod(P * s, WA_COLS)
+            cols = slice(HALF * h, HALF * (h + 1))
+            a_ps = psum.tile([P, HALF], F32, name="a_ps", tag="a")
+            for a in range(2):
+                w0 = WA_COLS * a + c0
+                nc.tensor.matmul_mx(
+                    out=a_ps[:],
+                    lhsT=wa_codes[q][:, w0:w0 + P].bitcast(FP8X4), lhsT_scale=wa_scales[q][:, w0:w0 + P],
+                    rhs=vw[a][:, cols].bitcast(FP8X4), rhs_scale=vs[4 * (a + 1):P, cols],
+                    start=(a == 0), stop=(a == 1))
+            a_sb = work.tile([P, HALF], F32, name="a_sb", bufs=6)
+            nc.vector.tensor_tensor(a_sb[:], a_ps[:], sit_sb[s][:, cols], ALU.mult)
+            a_of[s, h] = a_sb
+
+        def summed_transposes(s, c0, width, t_sb):
+            h, a0 = divmod(c0, HALF)
+            nc.vector.scalar_tensor_tensor(
+                t_sb, a_of[s, h][:, a0:a0 + width], gz_sb[:, s:s + 1], pages[PAGE_OF[s]][:, c0:c0 + width],
+                ALU.add, ALU.mult)
+            zt_ps = psum.tile([P, width // P, P], F32, name="zt_ps", tag="tr")
+            for jt in range(width // P):
+                nc.tensor.matmul(zt_ps[:, jt, :], a_of[s, h][:, a0 + P * jt:a0 + P * (jt + 1)], ident[:],
+                                 start=True, stop=False, is_transpose=True)
+                nc.tensor.matmul(zt_ps[:, jt, :], t_sb[:, P * jt:P * (jt + 1)], ident[:],
+                                 start=False, stop=True, is_transpose=True)
+            return zt_ps
+
+        def round_out(s, quarter, src):
+            b, ss = divmod(s, 4)
+            if ss == 0:
+                zt[b, quarter] = work.tile([P, 2, 2, 2 * P], BF16, name="zt_sb", bufs=6)
+            nc.scalar.copy(
+                zt[b, quarter][:, :, :, 64 * ss:64 * (ss + 1)].rearrange("p u jt (m e) -> p u jt m e", e=2),
+                src.rearrange("p jt (m u e) -> p u jt m e", u=2, e=2))
+
+        def combine(s, h):
+            zt_ps = summed_transposes(s, HALF * h, HALF, sit_sb[s + 1][:, HALF * h:HALF * (h + 1)])
+            for q in range(2):
+                round_out(s, 2 * h + q, zt_ps[:, 2 * q:2 * q + 2, :])
+
+        def combine_last(quarter):
+            t_sb = work.tile([P, QUARTER], F32, name="t_sb", bufs=4)
+            zt_ps = summed_transposes(SLICES - 1, QUARTER * quarter, QUARTER, t_sb[:])
+            round_out(SLICES - 1, quarter, zt_ps[:])
+
+        def turn_words(b, quarter, zi_words, copy):
+            words = zt[b, quarter][:].rearrange("p u jt c -> p (u jt c)").bitcast(F32)
+            w_ps = psum.tile([P, 2, 2, P], F32, name="w_ps", tag="tr")
+            for jj in range(2):
+                for u in range(2):
+                    w0 = P * (2 * u + jj)
+                    nc.tensor.transpose(w_ps[:, jj, u, :], words[:, w0:w0 + P], ident[:])
+            copy(zi_words.rearrange("p (jj j u) -> p jj j u", jj=2, u=2), w_ps[:].rearrange("p jj u j -> p jj j u"))
+
+        def quantise_first(h):
+            zi = work.tile([P, 4 * HALF], BF16, name="zi", align_bytes=64)
+            for q in range(2):
+                turn_words(0, 2 * h + q, zi[:].bitcast(F32)[:, HALF * q:HALF * (q + 1)], nc.scalar.copy)
+            nc.vector.quantize_mx(out=z_codes[0][h][:].bitcast(FP8X4), scales=z_scales[0][h][:], in_=zi[:])
+
+        def quantise_second(quarter):
+            h, q = divmod(quarter, 2)
+            cols = slice(QUARTER * q, QUARTER * (q + 1))
+            ziq = work.tile([P, 4 * QUARTER], BF16, name="ziq", tag="big", bufs=3, align_bytes=64)
+            turn_words(1, quarter, ziq[:].bitcast(F32), nc.vector.tensor_copy)
+            nc.vector.quantize_mx(out=z_codes[1][h][:, cols].bitcast(FP8X4), scales=z_scales[1][h][:, cols], in_=ziq[:])
+
+        y_of = {}
+
+        def open_sum(h, nt, tag):
+            y_ps = psum.tile([P, HALF], F32, name="y_ps", tag=tag, bufs=BANKS[tag])
+            y_of[h, nt] = y_ps
+            nc.tensor.matmul_mx(
+                out=y_ps[:],
+                lhsT=wo_codes[:, P * nt:P * (nt + 1)].bitcast(FP8X4), lhsT_scale=wo_scales[:, P * nt:P * (nt + 1)],
+                rhs=z_codes[0][h][:].bitcast(FP8X4), rhs_scale=z_scales[0][h][:],
+                start=True, stop=False)
+
+        def add_second(quarter):
+            h, q = divmod(quarter, 2)
+            cols = slice(QUARTER * q, QUARTER * (q + 1))
+            for nt in range(N // P):
+                w0 = N + P * nt
+                nc.tensor.matmul_mx(
+                    out=y_of[h, nt][:, cols],
+                    lhsT=wo_codes[:, w0:w0 + P].bitcast(FP8X4), lhsT_scale=wo_scales[:, w0:w0 + P],
+                    rhs=z_codes[1][h][:, cols].bitcast(FP8X4), rhs_scale=z_scales[1][h][:, cols],
+                    start=False, stop=(q == 1))
+
+        def read_out(h):
+            for nt in range(N // P):
+                o_sb = work.tile([P, HALF], F32, name="o_sb", tag="wa_raw", bufs=4)
+                nc.scalar.activation(o_sb[:], y_of[h, nt][:], ACT.Sigmoid)
+                nc.sync.dma_start(out[P * nt:P * (nt + 1), HALF * h:HALF * (h + 1)], o_sb[:])
+
+        def finish(quarter):
+            quantise_second(quarter)
+            if quarter == 2:
+                open_sum(1, 2, "a")
+            add_second(quarter)
+            if quarter % 2 == 1:
+                read_out(quarter // 2)
+
+        for q in range(4):
+            load_wa(q)
+            load_sit(2 * q)
+            load_sit(2 * q + 1)
+            if q == 1:
+                load_wo()
+
+        c_tags = ("co", "co", "a", "a", "a", "tr", "tr", "tr")
+        measure(0, c_tags[0])
+        nc.vector.tensor_copy(vs[:], ts[:].indirect(offs_sb[:]))
+        for s in range(1, SLICES):
+            measure(s, c_tags[s])
+        place(0)
+        nc.vector.tensor_copy(vw[0][:], tw[0][:].bitcast(U32).indirect(offs_sb[:]))
+        place(1)
+        nc.vector.tensor_copy(vw[1][:], tw[1][:].bitcast(U32).indirect(offs_sb[:]))
+        quantise_wa(0)
+        frames(0, 0)
+        frames(0, 1)
+        for s in range(SLICES - 1):
+            nxt = s + 1
+            if nxt % 2 == 0:
+                quantise_wa(nxt // 2)
+            if s == 4:
+                quantise_wo()
+            frames(nxt, 0)
+            frames(nxt, 1)
+            combine(s, 0)
+            combine(s, 1)
+            if s == 0:
+                place(2)
+            elif s >= 2:
+                place(nxt)
+            if s == 3:
+                quantise_first(0)
+                quantise_first(1)
+        for nt in range(3):
+            open_sum(0, nt, "a")
+        for nt in range(2):
+            open_sum(1, nt, "co")
+        for quarter in range(4):
+            combine_last(quarter)
+            if quarter >= 1:
+                finish(quarter - 1)
+        finish(3)

@@ -21,9 +21,11 @@ P = 128
 PASS = 512
 SLICES = H // P
 HALF = 512
-PAGE_OF = (0, 1, 0, 0, 0, 0, 0, 0)
+PAGE_OF = (0, 1, 2, 1, 1, 1, 1, 1)
 WA_COLS = 256
 QUARTER = 256
+WC_FIRST = 256
+DIRECT = 3
 BANKS = {"co": 2, "a": 3, "tr": 3}
 
 
@@ -45,12 +47,13 @@ def tile_list_band_comfort_predictor_kernel(
         t2s = keep.tile([P, 3, TB], U8, name="t2s", align_bytes=64)
         wcs = keep.tile([P, 3, H], U8, name="wcs", align_bytes=64)
         ts = keep.tile([P, T], U8, name="ts", align_bytes=64)
-        wcw = keep.tile([P, 3, 2 * H], U8, name="wcw", align_bytes=64)
+        wcw_first = keep.tile([P, 3, 2 * WC_FIRST], U8, name="wcw_first", align_bytes=64)
+        wcw_rest = keep.tile([P, 3, 2 * (H - WC_FIRST)], U8, name="wcw_rest", align_bytes=64)
         wgs_sb = keep.tile([P, NP], F32, name="wgs_sb")
         ident = keep.tile([P, P], F32, name="ident")
         gz_rows = keep.tile([P, P], F32, name="gz_rows")
         gz_sb = keep.tile([P, SLICES], F32, name="gz_sb")
-        pages = [keep.tile([P, S], F32, name="page%d" % i) for i in range(2)]
+        pages = [keep.tile([P, S], F32, name="page%d" % i) for i in range(3)]
         v2w = [keep.tile([P, NP], U32, name="v2w%d" % a, align_bytes=64) for a in range(3)]
         v2s = [keep.tile([P, NP], U8, name="v2s%d" % a, align_bytes=64) for a in range(3)]
         vw = [keep.tile([P, S], U32, name="vw%d" % a, align_bytes=64) for a in range(2)]
@@ -72,34 +75,34 @@ def tile_list_band_comfort_predictor_kernel(
         nc.gpsimd.memset(gz_rows[:], 0.0)
         make_identity(nc, ident[:])
 
+        t2w = [work.tile([P, TB], I32, name="t2w%d" % a, tag="big", bufs=3, align_bytes=64) for a in range(3)]
+
+        def load_words(dst, src):
+            nc.sync.dma_start(dst[:], src.rearrange("p t i -> p (t i)").bitcast(I32))
+
+        def load_planes(dst, src):
+            for r in range(4):
+                nc.sync.dma_start(
+                    dst[r:P:32, :, :].bitcast(I32),
+                    src.rearrange("a (q r) t -> r q a t", r=4)[r].bitcast(I32))
+
         nc.sync.dma_start(offs2_sb[:], offs2)
-        for q in range(4):
-            nc.sync.dma_start(
-                t2s[32 * q:32 * q + 4, :, :].bitcast(I32),
-                tab2_scales[:, 4 * q:4 * q + 4, :].rearrange("a r t -> r a t").bitcast(I32))
         nc.sync.dma_start(pos_sb[:], pos1)
         nc.sync.dma_start(offs_sb[:], offs)
+        load_words(t2w[0], tab2_words[0])
         nc.sync.dma_start(gz_rows[0:SLICES, :], gz.rearrange("(s p) -> s p", p=P))
-        t2w = []
-        for a in range(3):
-            t2w_a = work.tile([P, TB], I32, name="t2w%d" % a, tag="big", bufs=3, align_bytes=64)
-            t2w.append(t2w_a)
-            words = tab2_words[a].rearrange("p t i -> p (t i)").bitcast(I32)
-            width = TB // (4, 2, 1)[a]
-            for c0 in range(0, TB, width):
-                nc.sync.dma_start(t2w_a[:, c0:c0 + width], words[:, c0:c0 + width])
+        load_planes(t2s, tab2_scales)
+        load_words(t2w[1], tab2_words[1])
+        load_planes(wcs, wc_scales)
+        wc_rows = wc_words.rearrange("a p n -> p a n")
+        nc.sync.dma_start(wcw_first[:].bitcast(I32), wc_rows[:, :, 0:2 * WC_FIRST].bitcast(I32))
+        load_words(t2w[2], tab2_words[2])
+        nc.sync.dma_start(wgs_sb[:], wgs)
+        nc.sync.dma_start(wcw_rest[:].bitcast(I32), wc_rows[:, :, 2 * WC_FIRST:2 * H].bitcast(I32))
         for q in range(4):
             nc.sync.dma_start(
-                wcs[32 * q:32 * q + 4, :, :].bitcast(I32),
-                wc_scales[:, 4 * q:4 * q + 4, :].rearrange("a r t -> r a t").bitcast(I32))
-        for q in range(4):
-            nc.gpsimd.dma_start(
                 ts[32 * q + 4:32 * q + 12, :].bitcast(I32),
                 tab_scales[:, 4 * q:4 * q + 4, :].bitcast(I32))
-        nc.sync.dma_start(wcw[:].bitcast(I32), wc_words.rearrange("a p n -> p a n").bitcast(I32))
-        nc.sync.dma_start(wgs_sb[:], wgs)
-        for a in range(2):
-            nc.sync.dma_start(tw[a][:], tab_words[a].rearrange("p t i -> p (t i)").bitcast(I32))
 
         gz_ps = psum.tile([P, P], F32, name="gz_ps", tag="tr")
         nc.tensor.transpose(gz_ps[:], gz_rows[:], ident[:])
@@ -153,18 +156,45 @@ def tile_list_band_comfort_predictor_kernel(
 
         b_of = {}
 
-        def measure(s, tag):
+        def wc_operand(s, a):
+            c0 = P * s
+            words = wcw_first if c0 < WC_FIRST else wcw_rest
+            w0 = 2 * (c0 if c0 < WC_FIRST else c0 - WC_FIRST)
+            return words[:, a, w0:w0 + 2 * P].bitcast(FP4X4), wcs[:, a, c0:c0 + P]
+
+        def measure_direct(s, tag):
             c_ps = psum.tile([P, NP], F32, name="c_ps", tag=tag, bufs=BANKS[tag])
             for a in range(3):
+                words, scales = wc_operand(s, a)
                 nc.tensor.matmul_mx(
-                    out=c_ps[:],
-                    lhsT=wcw[:, a, 2 * P * s:2 * P * (s + 1)].bitcast(FP4X4),
-                    lhsT_scale=wcs[:, a, P * s:P * (s + 1)],
+                    out=c_ps[:], lhsT=words, lhsT_scale=scales,
                     rhs=v2w[a][:].bitcast(FP8X4), rhs_scale=v2s[a][:],
                     start=(a == 0), stop=(a == 2))
             b_sb = keep.tile([P, NP], F32, name="b_sb%d" % s)
             nc.scalar.activation(b_sb[:], c_ps[:], ACT.Gelu_apprx_tanh)
             nc.vector.tensor_tensor(b_sb[:], c_ps[:], b_sb[:], ALU.add)
+            b_of[s] = b_sb
+
+        def measure_turned(s, tag):
+            ct_ps = psum.tile([P, NP], F32, name="ct_ps", tag=tag, bufs=BANKS[tag])
+            for jt in range(NP // P):
+                js = slice(P * jt, P * (jt + 1))
+                for a in range(3):
+                    words, scales = wc_operand(s, a)
+                    nc.tensor.matmul_mx(
+                        out=ct_ps[:, js], lhsT=v2w[a][:, js].bitcast(FP8X4), lhsT_scale=v2s[a][:, js],
+                        rhs=words, rhs_scale=scales, start=(a == 0), stop=(a == 2))
+            gt_sb = work.tile([P, NP], F32, name="gt_sb", tag="a_sb", bufs=6)
+            nc.scalar.activation(gt_sb[:], ct_ps[:], ACT.Gelu_apprx_tanh)
+            ct_sb = work.tile([P, NP], F32, name="ct_sb", tag="a_sb", bufs=6)
+            nc.scalar.copy(ct_sb[:], ct_ps[:])
+            b_ps = psum.tile([P, NP], F32, name="b_ps", tag="tr")
+            for jt in range(NP // P):
+                js = slice(P * jt, P * (jt + 1))
+                nc.tensor.matmul(b_ps[:, js], gt_sb[:, js], ident[:], start=True, stop=False, is_transpose=True)
+                nc.tensor.matmul(b_ps[:, js], ct_sb[:, js], ident[:], start=False, stop=True, is_transpose=True)
+            b_sb = keep.tile([P, NP], F32, name="b_sb%d" % s)
+            nc.scalar.copy(b_sb[:], b_ps[:])
             b_of[s] = b_sb
 
         def place(s):
@@ -185,7 +215,7 @@ def tile_list_band_comfort_predictor_kernel(
                     lhsT=wa_codes[q][:, w0:w0 + P].bitcast(FP8X4), lhsT_scale=wa_scales[q][:, w0:w0 + P],
                     rhs=vw[a][:, cols].bitcast(FP8X4), rhs_scale=vs[4 * (a + 1):P, cols],
                     start=(a == 0), stop=(a == 1))
-            a_sb = work.tile([P, HALF], F32, name="a_sb", bufs=6)
+            a_sb = work.tile([P, HALF], F32, name="a_sb", tag="a_sb", bufs=6)
             nc.vector.tensor_tensor(a_sb[:], a_ps[:], sit_sb[s][:, cols], ALU.mult)
             a_of[s, h] = a_sb
 
@@ -196,9 +226,9 @@ def tile_list_band_comfort_predictor_kernel(
                 ALU.add, ALU.mult)
             zt_ps = psum.tile([P, width // P, P], F32, name="zt_ps", tag="tr")
             for jt in range(width // P):
-                nc.tensor.matmul(zt_ps[:, jt, :], a_of[s, h][:, a0 + P * jt:a0 + P * (jt + 1)], ident[:],
-                                 start=True, stop=False, is_transpose=True)
                 nc.tensor.matmul(zt_ps[:, jt, :], t_sb[:, P * jt:P * (jt + 1)], ident[:],
+                                 start=True, stop=False, is_transpose=True)
+                nc.tensor.matmul(zt_ps[:, jt, :], a_of[s, h][:, a0 + P * jt:a0 + P * (jt + 1)], ident[:],
                                  start=False, stop=True, is_transpose=True)
             return zt_ps
 
@@ -220,9 +250,9 @@ def tile_list_band_comfort_predictor_kernel(
             zt_ps = summed_transposes(SLICES - 1, QUARTER * quarter, QUARTER, t_sb[:])
             round_out(SLICES - 1, quarter, zt_ps[:])
 
-        def turn_words(b, quarter, zi_words, copy):
+        def turn_words(b, quarter, zi_words, copy, tag):
             words = zt[b, quarter][:].rearrange("p u jt c -> p (u jt c)").bitcast(F32)
-            w_ps = psum.tile([P, 2, 2, P], F32, name="w_ps", tag="tr")
+            w_ps = psum.tile([P, 2, 2, P], F32, name="w_ps", tag=tag, bufs=BANKS[tag])
             for jj in range(2):
                 for u in range(2):
                     w0 = P * (2 * u + jj)
@@ -232,14 +262,14 @@ def tile_list_band_comfort_predictor_kernel(
         def quantise_first(h):
             zi = work.tile([P, 4 * HALF], BF16, name="zi", align_bytes=64)
             for q in range(2):
-                turn_words(0, 2 * h + q, zi[:].bitcast(F32)[:, HALF * q:HALF * (q + 1)], nc.scalar.copy)
+                turn_words(0, 2 * h + q, zi[:].bitcast(F32)[:, HALF * q:HALF * (q + 1)], nc.scalar.copy, "tr")
             nc.vector.quantize_mx(out=z_codes[0][h][:].bitcast(FP8X4), scales=z_scales[0][h][:], in_=zi[:])
 
         def quantise_second(quarter):
             h, q = divmod(quarter, 2)
             cols = slice(QUARTER * q, QUARTER * (q + 1))
             ziq = work.tile([P, 4 * QUARTER], BF16, name="ziq", tag="big", bufs=3, align_bytes=64)
-            turn_words(1, quarter, ziq[:].bitcast(F32), nc.vector.tensor_copy)
+            turn_words(1, quarter, ziq[:].bitcast(F32), nc.vector.tensor_copy, "co")
             nc.vector.quantize_mx(out=z_codes[1][h][:, cols].bitcast(FP8X4), scales=z_scales[1][h][:, cols], in_=ziq[:])
 
         y_of = {}
@@ -266,58 +296,69 @@ def tile_list_band_comfort_predictor_kernel(
 
         def read_out(h):
             for nt in range(N // P):
-                o_sb = work.tile([P, HALF], F32, name="o_sb", tag="wa_raw", bufs=4)
+                o_sb = work.tile([P, HALF], F32, name="o_sb", tag="sit", bufs=6)
                 nc.scalar.activation(o_sb[:], y_of[h, nt][:], ACT.Sigmoid)
                 nc.sync.dma_start(out[P * nt:P * (nt + 1), HALF * h:HALF * (h + 1)], o_sb[:])
 
         def finish(quarter):
             quantise_second(quarter)
             if quarter == 2:
-                open_sum(1, 2, "a")
+                for nt in range(N // P):
+                    open_sum(1, nt, "a")
             add_second(quarter)
             if quarter % 2 == 1:
                 read_out(quarter // 2)
 
-        for q in range(4):
-            load_wa(q)
-            load_sit(2 * q)
-            load_sit(2 * q + 1)
-            if q == 1:
-                load_wo()
+        load_wa(0)
+        load_words(tw[0], tab_words[0])
+        load_words(tw[1], tab_words[1])
+        load_wa(1)
+        load_sit(0)
+        load_sit(1)
+        load_wa(2)
+        load_sit(2)
+        load_sit(3)
+        load_wa(3)
+        load_sit(4)
+        load_sit(5)
+        load_wo()
+        load_sit(6)
+        load_sit(7)
 
-        c_tags = ("co", "co", "a", "a", "a", "tr", "tr", "tr")
-        measure(0, c_tags[0])
-        nc.vector.tensor_copy(vs[:], ts[:].indirect(offs_sb[:]))
-        for s in range(1, SLICES):
-            measure(s, c_tags[s])
+        c_tags = ("co", "co", "a", "a", "a", "co", "co", "a")
+        for s in range(SLICES):
+            if s < DIRECT:
+                measure_direct(s, c_tags[s])
+            else:
+                measure_turned(s, c_tags[s])
         place(0)
-        nc.vector.tensor_copy(vw[0][:], tw[0][:].bitcast(U32).indirect(offs_sb[:]))
         place(1)
-        nc.vector.tensor_copy(vw[1][:], tw[1][:].bitcast(U32).indirect(offs_sb[:]))
+        nc.vector.tensor_copy(vs[:], ts[:].indirect(offs_sb[:]))
+        nc.vector.tensor_copy(vw[0][:], tw[0][:].bitcast(U32).indirect(offs_sb[:]))
+        place(2)
         quantise_wa(0)
+        for h in range(2):
+            nc.vector.tensor_copy(
+                vw[1][:, HALF * h:HALF * (h + 1)], tw[1][:].bitcast(U32).indirect(offs_sb[:, 32 * h:32 * (h + 1)]))
         frames(0, 0)
         frames(0, 1)
+        next_on_page = {1:[3],3:[4],4:[5],5:[6],6:[7]}
         for s in range(SLICES - 1):
-            nxt = s + 1
-            if nxt % 2 == 0:
-                quantise_wa(nxt // 2)
-            if s == 4:
+            if s in (0, 2, 4):
+                quantise_wa(s // 2 + 1)
+            if s == 5:
                 quantise_wo()
-            frames(nxt, 0)
-            frames(nxt, 1)
+            frames(s + 1, 0)
+            frames(s + 1, 1)
             combine(s, 0)
             combine(s, 1)
-            if s == 0:
-                place(2)
-            elif s >= 2:
-                place(nxt)
+            for k in next_on_page.get(s, ()):
+                place(k)
             if s == 3:
                 quantise_first(0)
                 quantise_first(1)
         for nt in range(3):
             open_sum(0, nt, "a")
-        for nt in range(2):
-            open_sum(1, nt, "co")
         for quarter in range(4):
             combine_last(quarter)
             if quarter >= 1:

@@ -25,7 +25,7 @@ PAGE_OF = (0, 1, 2, 1, 1, 1, 1, 1)
 WA_COLS = 256
 QUARTER = 256
 WC_FIRST = 256
-DIRECT = 3
+DIRECT = 4
 BANKS = {"co": 2, "a": 3, "tr": 3}
 
 
@@ -51,11 +51,13 @@ def tile_list_band_comfort_predictor_kernel(
         wcw_rest = keep.tile([P, 3, 2 * (H - WC_FIRST)], U8, name="wcw_rest", align_bytes=64)
         wgs_sb = keep.tile([P, NP], F32, name="wgs_sb")
         ident = keep.tile([P, P], F32, name="ident")
-        gz_rows = keep.tile([P, P], F32, name="gz_rows")
+        gz_rows = work.tile([P, P], F32, name="gz_rows", tag="t_sb", bufs=4)
         gz_sb = keep.tile([P, SLICES], F32, name="gz_sb")
         pages = [keep.tile([P, S], F32, name="page%d" % i) for i in range(3)]
         v2w = [keep.tile([P, NP], U32, name="v2w%d" % a, align_bytes=64) for a in range(3)]
-        v2s = [keep.tile([P, NP], U8, name="v2s%d" % a, align_bytes=64) for a in range(3)]
+        v2s_picked = keep.tile([P, 3, NP], U8, name="v2s_picked", align_bytes=64)
+        v2s = keep.tile([P, 3 * NP], U8, name="v2s", align_bytes=64)
+        vs_picked = keep.tile([P, S], U8, name="vs_picked", align_bytes=64)
         vw = [keep.tile([P, S], U32, name="vw%d" % a, align_bytes=64) for a in range(2)]
         vs = keep.tile([P, S], U8, name="vs", align_bytes=64)
         tw = [keep.tile([P, T], I32, name="tw%d" % a, align_bytes=64) for a in range(2)]
@@ -70,6 +72,8 @@ def tile_list_band_comfort_predictor_kernel(
         nc.vector.memset(t2s[:].rearrange("p a t -> p (a t)").bitcast(I32), 0)
         nc.vector.memset(wcs[:].rearrange("p a t -> p (a t)").bitcast(I32), 0)
         nc.vector.memset(ts[:].bitcast(I32), 0)
+        nc.vector.memset(v2s[:].bitcast(I32), 0)
+        nc.vector.memset(vs[:].bitcast(I32), 0)
         for page in pages:
             nc.vector.memset(page[:], 0.0)
         nc.gpsimd.memset(gz_rows[:], 0.0)
@@ -91,27 +95,38 @@ def tile_list_band_comfort_predictor_kernel(
         nc.sync.dma_start(offs_sb[:], offs)
         load_words(t2w[0], tab2_words[0])
         nc.sync.dma_start(gz_rows[0:SLICES, :], gz.rearrange("(s p) -> s p", p=P))
-        load_planes(t2s, tab2_scales)
+        nc.sync.dma_start(t2s[0:P:8, :, :].bitcast(I32), tab2_scales.rearrange("a q t -> q a t").bitcast(I32))
         load_words(t2w[1], tab2_words[1])
         load_planes(wcs, wc_scales)
         wc_rows = wc_words.rearrange("a p n -> p a n")
         nc.sync.dma_start(wcw_first[:].bitcast(I32), wc_rows[:, :, 0:2 * WC_FIRST].bitcast(I32))
         load_words(t2w[2], tab2_words[2])
-        nc.sync.dma_start(wgs_sb[:], wgs)
-        nc.sync.dma_start(wcw_rest[:].bitcast(I32), wc_rows[:, :, 2 * WC_FIRST:2 * H].bitcast(I32))
-        for q in range(4):
-            nc.sync.dma_start(
-                ts[32 * q + 4:32 * q + 12, :].bitcast(I32),
-                tab_scales[:, 4 * q:4 * q + 4, :].bitcast(I32))
+        nc.sync.dma_start(ts[0:P:4, :].bitcast(I32), tab_scales.rearrange("a q t -> (a q) t").bitcast(I32))
 
         gz_ps = psum.tile([P, P], F32, name="gz_ps", tag="tr")
         nc.tensor.transpose(gz_ps[:], gz_rows[:], ident[:])
         nc.scalar.copy(gz_sb[:], gz_ps[:, 0:SLICES])
 
         for a in range(3):
-            nc.vector.tensor_copy(v2s[a][:], t2s[:, a, :].indirect(offs2_sb[:]))
+            nc.vector.tensor_copy(v2s_picked[:, a, :], t2s[:, a, :].indirect(offs2_sb[:]))
+        for r in range(4):
+            nc.sync.dma_start(
+                v2s[r:P:32, :].bitcast(I32),
+                v2s_picked[8 * r:P:32, :, :].rearrange("p a j -> p (a j)").bitcast(I32))
         for a in range(3):
             nc.vector.tensor_copy(v2w[a][:], t2w[a][:].bitcast(U32).indirect(offs2_sb[:]))
+        nc.vector.tensor_copy(vs_picked[:], ts[:].indirect(offs_sb[:]))
+        nc.sync.dma_start(wgs_sb[:], wgs)
+        nc.sync.dma_start(wcw_rest[:].bitcast(I32), wc_rows[:, :, 2 * WC_FIRST:2 * H].bitcast(I32))
+
+        def move_planes(a):
+            for r in range(4):
+                nc.sync.dma_start(
+                    vs[4 * (a + 1) + r:P:32, :].bitcast(I32),
+                    vs_picked[64 * a + 4 * r:64 * (a + 1):16, :].bitcast(I32))
+
+        gt_sb = work.tile([P, 4, HALF], F32, name="gt_sb", tag="big", bufs=3, align_bytes=64)
+        ct_sb = work.tile([P, 4, HALF], F32, name="ct_sb", tag="big", bufs=3, align_bytes=64)
 
         sit_sb = {}
         wa_raw = {}
@@ -168,34 +183,37 @@ def tile_list_band_comfort_predictor_kernel(
                 words, scales = wc_operand(s, a)
                 nc.tensor.matmul_mx(
                     out=c_ps[:], lhsT=words, lhsT_scale=scales,
-                    rhs=v2w[a][:].bitcast(FP8X4), rhs_scale=v2s[a][:],
+                    rhs=v2w[a][:].bitcast(FP8X4), rhs_scale=v2s[:, NP * a:NP * (a + 1)],
                     start=(a == 0), stop=(a == 2))
             b_sb = keep.tile([P, NP], F32, name="b_sb%d" % s)
             nc.scalar.activation(b_sb[:], c_ps[:], ACT.Gelu_apprx_tanh)
             nc.vector.tensor_tensor(b_sb[:], c_ps[:], b_sb[:], ALU.add)
             b_of[s] = b_sb
 
-        def measure_turned(s, tag):
-            ct_ps = psum.tile([P, NP], F32, name="ct_ps", tag=tag, bufs=BANKS[tag])
+        def measure_turned():
+            r0 = P * DIRECT
+            w0 = 2 * (r0 - WC_FIRST)
             for jt in range(NP // P):
-                js = slice(P * jt, P * (jt + 1))
+                ct_ps = psum.tile([P, HALF], F32, name="ct_ps", tag="a")
                 for a in range(3):
-                    words, scales = wc_operand(s, a)
+                    j0 = P * jt
                     nc.tensor.matmul_mx(
-                        out=ct_ps[:, js], lhsT=v2w[a][:, js].bitcast(FP8X4), lhsT_scale=v2s[a][:, js],
-                        rhs=words, rhs_scale=scales, start=(a == 0), stop=(a == 2))
-            gt_sb = work.tile([P, NP], F32, name="gt_sb", tag="a_sb", bufs=6)
-            nc.scalar.activation(gt_sb[:], ct_ps[:], ACT.Gelu_apprx_tanh)
-            ct_sb = work.tile([P, NP], F32, name="ct_sb", tag="a_sb", bufs=6)
-            nc.scalar.copy(ct_sb[:], ct_ps[:])
-            b_ps = psum.tile([P, NP], F32, name="b_ps", tag="tr")
-            for jt in range(NP // P):
-                js = slice(P * jt, P * (jt + 1))
-                nc.tensor.matmul(b_ps[:, js], gt_sb[:, js], ident[:], start=True, stop=False, is_transpose=True)
-                nc.tensor.matmul(b_ps[:, js], ct_sb[:, js], ident[:], start=False, stop=True, is_transpose=True)
-            b_sb = keep.tile([P, NP], F32, name="b_sb%d" % s)
-            nc.scalar.copy(b_sb[:], b_ps[:])
-            b_of[s] = b_sb
+                        out=ct_ps[:], lhsT=v2w[a][:, j0:j0 + P].bitcast(FP8X4),
+                        lhsT_scale=v2s[:, NP * a + j0:NP * a + j0 + P],
+                        rhs=wcw_rest[:, a, w0:w0 + 2 * HALF].bitcast(FP4X4), rhs_scale=wcs[:, a, r0:r0 + HALF],
+                        start=(a == 0), stop=(a == 2))
+                nc.scalar.activation(gt_sb[:, jt, :], ct_ps[:], ACT.Gelu_apprx_tanh)
+                nc.scalar.copy(ct_sb[:, jt, :], ct_ps[:])
+            for s in range(DIRECT, SLICES):
+                rs = slice(P * (s - DIRECT), P * (s - DIRECT + 1))
+                b_ps = psum.tile([P, NP], F32, name="b_ps", tag="tr")
+                for jt in range(NP // P):
+                    js = slice(P * jt, P * (jt + 1))
+                    nc.tensor.matmul(b_ps[:, js], gt_sb[:, jt, rs], ident[:], start=True, stop=False, is_transpose=True)
+                    nc.tensor.matmul(b_ps[:, js], ct_sb[:, jt, rs], ident[:], start=False, stop=True, is_transpose=True)
+                b_sb = keep.tile([P, NP], F32, name="b_sb%d" % s)
+                nc.scalar.copy(b_sb[:], b_ps[:])
+                b_of[s] = b_sb
 
         def place(s):
             nc.vector.tensor_tensor(pages[PAGE_OF[s]][:].indirect(pos_sb[:]), b_of[s][:], wgs_sb[:], ALU.mult)
@@ -246,7 +264,7 @@ def tile_list_band_comfort_predictor_kernel(
                 round_out(s, 2 * h + q, zt_ps[:, 2 * q:2 * q + 2, :])
 
         def combine_last(quarter):
-            t_sb = work.tile([P, QUARTER], F32, name="t_sb", bufs=4)
+            t_sb = work.tile([P, QUARTER], F32, name="t_sb", tag="t_sb", bufs=4)
             zt_ps = summed_transposes(SLICES - 1, QUARTER * quarter, QUARTER, t_sb[:])
             round_out(SLICES - 1, quarter, zt_ps[:])
 
@@ -311,7 +329,9 @@ def tile_list_band_comfort_predictor_kernel(
 
         load_wa(0)
         load_words(tw[0], tab_words[0])
+        move_planes(0)
         load_words(tw[1], tab_words[1])
+        move_planes(1)
         load_wa(1)
         load_sit(0)
         load_sit(1)
@@ -321,19 +341,15 @@ def tile_list_band_comfort_predictor_kernel(
         load_wa(3)
         load_sit(4)
         load_sit(5)
+
+        for s in range(DIRECT):
+            measure_direct(s, "co")
+        measure_turned()
         load_wo()
         load_sit(6)
         load_sit(7)
-
-        c_tags = ("co", "co", "a", "a", "a", "co", "co", "a")
-        for s in range(SLICES):
-            if s < DIRECT:
-                measure_direct(s, c_tags[s])
-            else:
-                measure_turned(s, c_tags[s])
         place(0)
         place(1)
-        nc.vector.tensor_copy(vs[:], ts[:].indirect(offs_sb[:]))
         nc.vector.tensor_copy(vw[0][:], tw[0][:].bitcast(U32).indirect(offs_sb[:]))
         place(2)
         quantise_wa(0)

@@ -49,7 +49,7 @@ def tile_list_band_comfort_predictor_kernel(
         ts = keep.tile([P, T], U8, name="ts", align_bytes=64)
         wcw_first = keep.tile([P, 3, 2 * WC_FIRST], U8, name="wcw_first", align_bytes=64)
         wcw_rest = keep.tile([P, 3, 2 * (H - WC_FIRST)], U8, name="wcw_rest", align_bytes=64)
-        wgs_sb = keep.tile([P, NP], F32, name="wgs_sb")
+        wgs_sb = keep.tile([P, NP], F32, name="wgs_sb", tag="wgs", align_bytes=64)
         ident = keep.tile([P, P], F32, name="ident")
         gz_rows = work.tile([P, P], F32, name="gz_rows", tag="t_sb", bufs=4)
         gz_sb = keep.tile([P, SLICES], F32, name="gz_sb")
@@ -64,9 +64,11 @@ def tile_list_band_comfort_predictor_kernel(
         wa_codes = [keep.tile([P, 2 * WA_COLS], U32, name="wa_codes%d" % q, align_bytes=64) for q in range(4)]
         wa_scales = [keep.tile([P, 2 * WA_COLS], U8, name="wa_scales%d" % q, align_bytes=64) for q in range(4)]
         wo_bf = keep.tile([P, 2 * N * 4], BF16, name="wo_bf", align_bytes=64)
-        wo_codes = keep.tile([P, 2 * N], U32, name="wo_codes", align_bytes=64)
-        wo_scales = keep.tile([P, 2 * N], U8, name="wo_scales", align_bytes=64)
-        z_codes = [[keep.tile([P, HALF], U32, name="z_codes%d%d" % (b, h), align_bytes=64) for h in range(2)] for b in range(2)]
+        wo_codes = [keep.tile([P, N], U32, name="wo_codes0", align_bytes=64),
+                    keep.tile([P, N], U32, name="wo_codes1", tag="b_last", align_bytes=64)]
+        wo_scales = [keep.tile([P, N], U8, name="wo_scales%d" % b, align_bytes=64) for b in range(2)]
+        z_codes = [[keep.tile([P, HALF], U32, name="z_codes%d%d" % (b, h), align_bytes=64,
+                              tag="wgs" if (b, h) == (0, 1) else "z_codes%d%d" % (b, h)) for h in range(2)] for b in range(2)]
         z_scales = [[keep.tile([P, HALF], U8, name="z_scales%d%d" % (b, h), align_bytes=64) for h in range(2)] for b in range(2)]
 
         nc.vector.memset(t2s[:].rearrange("p a t -> p (a t)").bitcast(I32), 0)
@@ -162,12 +164,15 @@ def tile_list_band_comfort_predictor_kernel(
                 interleave(wa_bf[:, 4 * WA_COLS * a:4 * WA_COLS * (a + 1)], wa_raw[q, a][:])
             nc.vector.quantize_mx(out=wa_codes[q][:].bitcast(FP8X4), scales=wa_scales[q][:], in_=wa_bf[:])
 
-        def quantise_wo():
+        def round_wo():
             for b in range(2):
                 interleave(wo_bf[:, 4 * N * b:4 * N * (b + 1)], wo_raw[b][:])
-            for c0, c1 in ((0, 512), (512, 768)):
+
+        def quantise_wo(b):
+            for c0, c1 in ((0, 256), (256, N)):
                 nc.vector.quantize_mx(
-                    out=wo_codes[:, c0:c1].bitcast(FP8X4), scales=wo_scales[:, c0:c1], in_=wo_bf[:, 4 * c0:4 * c1])
+                    out=wo_codes[b][:, c0:c1].bitcast(FP8X4), scales=wo_scales[b][:, c0:c1],
+                    in_=wo_bf[:, 4 * (N * b + c0):4 * (N * b + c1)])
 
         b_of = {}
 
@@ -211,7 +216,8 @@ def tile_list_band_comfort_predictor_kernel(
                     js = slice(P * jt, P * (jt + 1))
                     nc.tensor.matmul(b_ps[:, js], gt_sb[:, jt, rs], ident[:], start=True, stop=False, is_transpose=True)
                     nc.tensor.matmul(b_ps[:, js], ct_sb[:, jt, rs], ident[:], start=False, stop=True, is_transpose=True)
-                b_sb = keep.tile([P, NP], F32, name="b_sb%d" % s)
+                b_sb = keep.tile([P, NP], F32, name="b_sb%d" % s, align_bytes=64,
+                                 tag="b_last" if s == SLICES - 1 else "b_sb%d" % s)
                 nc.scalar.copy(b_sb[:], b_ps[:])
                 b_of[s] = b_sb
 
@@ -277,11 +283,16 @@ def tile_list_band_comfort_predictor_kernel(
                     nc.tensor.transpose(w_ps[:, jj, u, :], words[:, w0:w0 + P], ident[:])
             copy(zi_words.rearrange("p (jj j u) -> p jj j u", jj=2, u=2), w_ps[:].rearrange("p jj u j -> p jj j u"))
 
-        def quantise_first(h):
+        zi_of = {}
+
+        def turn_first(h):
             zi = work.tile([P, 4 * HALF], BF16, name="zi", align_bytes=64)
+            zi_of[h] = zi
             for q in range(2):
                 turn_words(0, 2 * h + q, zi[:].bitcast(F32)[:, HALF * q:HALF * (q + 1)], nc.scalar.copy, "tr")
-            nc.vector.quantize_mx(out=z_codes[0][h][:].bitcast(FP8X4), scales=z_scales[0][h][:], in_=zi[:])
+
+        def quantise_first(h):
+            nc.vector.quantize_mx(out=z_codes[0][h][:].bitcast(FP8X4), scales=z_scales[0][h][:], in_=zi_of[h][:])
 
         def quantise_second(quarter):
             h, q = divmod(quarter, 2)
@@ -297,7 +308,7 @@ def tile_list_band_comfort_predictor_kernel(
             y_of[h, nt] = y_ps
             nc.tensor.matmul_mx(
                 out=y_ps[:],
-                lhsT=wo_codes[:, P * nt:P * (nt + 1)].bitcast(FP8X4), lhsT_scale=wo_scales[:, P * nt:P * (nt + 1)],
+                lhsT=wo_codes[0][:, P * nt:P * (nt + 1)].bitcast(FP8X4), lhsT_scale=wo_scales[0][:, P * nt:P * (nt + 1)],
                 rhs=z_codes[0][h][:].bitcast(FP8X4), rhs_scale=z_scales[0][h][:],
                 start=True, stop=False)
 
@@ -305,10 +316,10 @@ def tile_list_band_comfort_predictor_kernel(
             h, q = divmod(quarter, 2)
             cols = slice(QUARTER * q, QUARTER * (q + 1))
             for nt in range(N // P):
-                w0 = N + P * nt
+                w0 = P * nt
                 nc.tensor.matmul_mx(
                     out=y_of[h, nt][:, cols],
-                    lhsT=wo_codes[:, w0:w0 + P].bitcast(FP8X4), lhsT_scale=wo_scales[:, w0:w0 + P],
+                    lhsT=wo_codes[1][:, w0:w0 + P].bitcast(FP8X4), lhsT_scale=wo_scales[1][:, w0:w0 + P],
                     rhs=z_codes[1][h][:, cols].bitcast(FP8X4), rhs_scale=z_scales[1][h][:, cols],
                     start=False, stop=(q == 1))
 
@@ -363,7 +374,8 @@ def tile_list_band_comfort_predictor_kernel(
             if s in (0, 2, 4):
                 quantise_wa(s // 2 + 1)
             if s == 5:
-                quantise_wo()
+                round_wo()
+                quantise_wo(0)
             frames(s + 1, 0)
             frames(s + 1, 1)
             combine(s, 0)
@@ -371,12 +383,18 @@ def tile_list_band_comfort_predictor_kernel(
             for k in next_on_page.get(s, ()):
                 place(k)
             if s == 3:
+                turn_first(0)
                 quantise_first(0)
-                quantise_first(1)
+                turn_first(1)
         for nt in range(3):
             open_sum(0, nt, "a")
-        for quarter in range(4):
-            combine_last(quarter)
-            if quarter >= 1:
-                finish(quarter - 1)
+        combine_last(0)
+        combine_last(1)
+        quantise_wo(1)
+        finish(0)
+        combine_last(2)
+        finish(1)
+        combine_last(3)
+        quantise_first(1)
+        finish(2)
         finish(3)

from contextlib import ExitStack

import concourse.mybir as mybir
from concourse.masks import make_identity

K, T, S, K2, TB, NP, H, N = 1024, 4096, 1024, 1536, 2048, 512, 1024, 384
FLOPS = 2 * (K * H * S + K2 * H * NP + H * N * S)

F32 = mybir.dt.float32
BF16 = mybir.dt.bfloat16
I32 = mybir.dt.int32
U32 = mybir.dt.uint32
U16 = mybir.dt.uint16
U8 = mybir.dt.uint8
FP8X4 = mybir.dt.float8_e4m3fn_x4
FP4X4 = mybir.dt.float4_e2m1fn_x4
ACT = mybir.ActivationFunctionType
ALU = mybir.AluOpType

P = 128
PASS = 512
SLICES = H // P
HALF = 512
PAGE_OF = (0, 1, 2, 1, 1, 1, 1, 1)
WA_COLS = 256
QUARTER = 256
WC_FIRST = 256
DIRECT = 4
BANKS = {"co": 2, "a": 3, "tr": 3}


def tile_list_band_comfort_predictor_kernel(
    tc, tab_words, tab_scales, tab2_words, tab2_scales, offs, offs2, pos1,
    wa, wc_words, wc_scales, sit, wgs, gz, wo, out,
):
    nc = tc.nc
    with ExitStack() as ctx:
        lists = ctx.enter_context(tc.tile_pool(name="lists", bufs=1))
        keep = ctx.enter_context(tc.tile_pool(name="keep", bufs=1))
        work = ctx.enter_context(tc.tile_pool(name="work", bufs=2))
        psum = ctx.enter_context(tc.psum_pool(name="psum", bufs=3))

        offs_sb = lists.tile([P, S // 16], U16, name="offs_sb")
        offs2_sb = lists.tile([P, NP // 16], U16, name="offs2_sb")
        pos_sb = lists.tile([P, NP // 16], U16, name="pos_sb")

        t2s = keep.tile([P, 3, TB], U8, name="t2s", align_bytes=64)
        wcs = keep.tile([P, 3, H], U8, name="wcs", align_bytes=64)
        ts = keep.tile([P, T], U8, name="ts", align_bytes=64)
        wcw_first = keep.tile([P, 3, 2 * WC_FIRST], U8, name="wcw_first", align_bytes=64)
        wcw_rest = keep.tile([P, 3, 2 * (H - WC_FIRST)], U8, name="wcw_rest", align_bytes=64)
        wgs_sb = keep.tile([P, NP], F32, name="wgs_sb", tag="wgs", align_bytes=64)
        ident = keep.tile([P, P], F32, name="ident")
        gz_rows = work.tile([P, P], F32, name="gz_rows", tag="t_sb", bufs=4)
        gz_sb = keep.tile([P, SLICES], F32, name="gz_sb")
        pages = [keep.tile([P, S], F32, name="page%d" % i) for i in range(3)]
        v2w = [keep.tile([P, NP], U32, name="v2w%d" % a, align_bytes=64) for a in range(3)]
        v2s_picked = keep.tile([P, 3, NP], U8, name="v2s_picked", align_bytes=64)
        v2s = keep.tile([P, 3 * NP], U8, name="v2s", align_bytes=64)
        vs_picked = keep.tile([P, S], U8, name="vs_picked", align_bytes=64)
        vw = [keep.tile([P, S], U32, name="vw%d" % a, align_bytes=64) for a in range(2)]
        vs = keep.tile([P, S], U8, name="vs", align_bytes=64)
        tw = [keep.tile([P, T], I32, name="tw%d" % a, align_bytes=64) for a in range(2)]
        wa_codes = [keep.tile([P, 2 * WA_COLS], U32, name="wa_codes%d" % q, align_bytes=64) for q in range(4)]
        wa_scales = [keep.tile([P, 2 * WA_COLS], U8, name="wa_scales%d" % q, align_bytes=64) for q in range(4)]
        wo_bf = keep.tile([P, 2 * N * 4], BF16, name="wo_bf", align_bytes=64)
        wo_codes = [keep.tile([P, N], U32, name="wo_codes0", align_bytes=64),
                    keep.tile([P, N], U32, name="wo_codes1", tag="b_last", align_bytes=64)]
        wo_scales = [keep.tile([P, N], U8, name="wo_scales%d" % b, align_bytes=64) for b in range(2)]
        z_codes = [[keep.tile([P, HALF], U32, name="z_codes%d%d" % (b, h), align_bytes=64,
                              tag="wgs" if (b, h) == (0, 1) else "z_codes%d%d" % (b, h)) for h in range(2)] for b in range(2)]
        z_scales = [[keep.tile([P, HALF], U8, name="z_scales%d%d" % (b, h), align_bytes=64) for h in range(2)] for b in range(2)]

        nc.vector.memset(t2s[:].rearrange("p a t -> p (a t)").bitcast(I32), 0)
        nc.vector.memset(wcs[:].rearrange("p a t -> p (a t)").bitcast(I32), 0)
        nc.vector.memset(ts[:].bitcast(I32), 0)
        nc.vector.memset(v2s[:].bitcast(I32), 0)
        nc.vector.memset(vs[:].bitcast(I32), 0)
        for page in pages:
            nc.vector.memset(page[:], 0.0)
        nc.gpsimd.memset(gz_rows[:], 0.0)
        make_identity(nc, ident[:])

        t2w = [work.tile([P, TB], I32, name="t2w%d" % a, tag="big", bufs=3, align_bytes=64) for a in range(3)]

        def load_words(dst, src):
            nc.sync.dma_start(dst[:], src.rearrange("p t i -> p (t i)").bitcast(I32))

        def load_planes(dst, src):
            for r in range(4):
                nc.sync.dma_start(
                    dst[r:P:32, :, :].bitcast(I32),
                    src.rearrange("a (q r) t -> r q a t", r=4)[r].bitcast(I32))

        nc.sync.dma_start(offs2_sb[:], offs2)
        nc.sync.dma_start(pos_sb[:], pos1)
        nc.sync.dma_start(offs_sb[:], offs)
        load_words(t2w[0], tab2_words[0])
        nc.sync.dma_start(gz_rows[0:SLICES, :], gz.rearrange("(s p) -> s p", p=P))
        nc.sync.dma_start(t2s[0:P:8, :, :].bitcast(I32), tab2_scales.rearrange("a q t -> q a t").bitcast(I32))
        load_words(t2w[1], tab2_words[1])
        load_planes(wcs, wc_scales)
        wc_rows = wc_words.rearrange("a p n -> p a n")
        nc.sync.dma_start(wcw_first[:].bitcast(I32), wc_rows[:, :, 0:2 * WC_FIRST].bitcast(I32))
        load_words(t2w[2], tab2_words[2])
        nc.sync.dma_start(ts[0:P:4, :].bitcast(I32), tab_scales.rearrange("a q t -> (a q) t").bitcast(I32))

        gz_ps = psum.tile([P, P], F32, name="gz_ps", tag="tr")
        nc.tensor.transpose(gz_ps[:], gz_rows[:], ident[:])
        nc.scalar.copy(gz_sb[:], gz_ps[:, 0:SLICES])

        for a in range(3):
            nc.vector.tensor_copy(v2s_picked[:, a, :], t2s[:, a, :].indirect(offs2_sb[:]))
        for r in range(4):
            nc.sync.dma_start(
                v2s[r:P:32, :].bitcast(I32),
                v2s_picked[8 * r:P:32, :, :].rearrange("p a j -> p (a j)").bitcast(I32))
        for a in range(3):
            nc.vector.tensor_copy(v2w[a][:], t2w[a][:].bitcast(U32).indirect(offs2_sb[:]))
        nc.vector.tensor_copy(vs_picked[:], ts[:].indirect(offs_sb[:]))
        nc.sync.dma_start(wgs_sb[:], wgs)
        nc.sync.dma_start(wcw_rest[:].bitcast(I32), wc_rows[:, :, 2 * WC_FIRST:2 * H].bitcast(I32))

        def move_planes(a):
            for r in range(4):
                nc.sync.dma_start(
                    vs[4 * (a + 1) + r:P:32, :].bitcast(I32),
                    vs_picked[64 * a + 4 * r:64 * (a + 1):16, :].bitcast(I32))

        gt_sb = work.tile([P, 4, HALF], F32, name="gt_sb", tag="big", bufs=3, align_bytes=64)
        ct_sb = work.tile([P, 4, HALF], F32, name="ct_sb", tag="big", bufs=3, align_bytes=64)

        sit_sb = {}
        wa_raw = {}
        wo_raw = []

        def load_wa(q):
            for a in range(2):
                raw = work.tile([P, 4, WA_COLS], F32, name="wa_raw", tag="wa_raw", bufs=4)
                nc.sync.dma_start(
                    raw[:],
                    wa[PASS * a:PASS * (a + 1), WA_COLS * q:WA_COLS * (q + 1)].rearrange("(p i) c -> p i c", i=4))
                wa_raw[q, a] = raw

        def load_sit(s):
            tile = work.tile([P, S], F32, name="sit_sb", tag="sit", bufs=6)
            nc.sync.dma_start(tile[:], sit[P * s:P * (s + 1), :])
            sit_sb[s] = tile

        def load_wo():
            for b in range(2):
                raw = work.tile([P, 4, N], F32, name="wo_raw", tag="big", bufs=3, align_bytes=64)
                nc.sync.dma_start(raw[:], wo[PASS * b:PASS * (b + 1), :].rearrange("(p i) n -> p i n", i=4))
                wo_raw.append(raw)

        def interleave(dst, raw):
            nc.scalar.copy(
                dst.rearrange("p (c e i) -> p c i e", e=4, i=4),
                raw.rearrange("p i (c e) -> p c i e", e=4))

        def quantise_wa(q):
            wa_bf = work.tile([P, 2 * WA_COLS * 4], BF16, name="wa_bf", align_bytes=64)
            for a in range(2):
                interleave(wa_bf[:, 4 * WA_COLS * a:4 * WA_COLS * (a + 1)], wa_raw[q, a][:])
            nc.vector.quantize_mx(out=wa_codes[q][:].bitcast(FP8X4), scales=wa_scales[q][:], in_=wa_bf[:])

        def round_wo():
            for b in range(2):
                interleave(wo_bf[:, 4 * N * b:4 * N * (b + 1)], wo_raw[b][:])

        def quantise_wo(b):
            for c0, c1 in ((0, 256), (256, N)):
                nc.vector.quantize_mx(
                    out=wo_codes[b][:, c0:c1].bitcast(FP8X4), scales=wo_scales[b][:, c0:c1],
                    in_=wo_bf[:, 4 * (N * b + c0):4 * (N * b + c1)])

        b_of = {}

        def wc_operand(s, a):
            c0 = P * s
            words = wcw_first if c0 < WC_FIRST else wcw_rest
            w0 = 2 * (c0 if c0 < WC_FIRST else c0 - WC_FIRST)
            return words[:, a, w0:w0 + 2 * P].bitcast(FP4X4), wcs[:, a, c0:c0 + P]

        def measure_direct(s, tag):
            c_ps = psum.tile([P, NP], F32, name="c_ps", tag=tag, bufs=BANKS[tag])
            for a in range(3):
                words, scales = wc_operand(s, a)
                nc.tensor.matmul_mx(
                    out=c_ps[:], lhsT=words, lhsT_scale=scales,
                    rhs=v2w[a][:].bitcast(FP8X4), rhs_scale=v2s[:, NP * a:NP * (a + 1)],
                    start=(a == 0), stop=(a == 2))
            b_sb = keep.tile([P, NP], F32, name="b_sb%d" % s)
            nc.scalar.activation(b_sb[:], c_ps[:], ACT.Gelu_apprx_tanh)
            nc.vector.tensor_tensor(b_sb[:], c_ps[:], b_sb[:], ALU.add)
            b_of[s] = b_sb

        def measure_turned():
            r0 = P * DIRECT
            w0 = 2 * (r0 - WC_FIRST)
            for jt in range(NP // P):
                ct_ps = psum.tile([P, HALF], F32, name="ct_ps", tag="a")
                for a in range(3):
                    j0 = P * jt
                    nc.tensor.matmul_mx(
                        out=ct_ps[:], lhsT=v2w[a][:, j0:j0 + P].bitcast(FP8X4),
                        lhsT_scale=v2s[:, NP * a + j0:NP * a + j0 + P],
                        rhs=wcw_rest[:, a, w0:w0 + 2 * HALF].bitcast(FP4X4), rhs_scale=wcs[:, a, r0:r0 + HALF],
                        start=(a == 0), stop=(a == 2))
                nc.scalar.activation(gt_sb[:, jt, :], ct_ps[:], ACT.Gelu_apprx_tanh)
                nc.scalar.copy(ct_sb[:, jt, :], ct_ps[:])
            for s in range(DIRECT, SLICES):
                rs = slice(P * (s - DIRECT), P * (s - DIRECT + 1))
                b_ps = psum.tile([P, NP], F32, name="b_ps", tag="tr")
                for jt in range(NP // P):
                    js = slice(P * jt, P * (jt + 1))
                    nc.tensor.matmul(b_ps[:, js], gt_sb[:, jt, rs], ident[:], start=True, stop=False, is_transpose=True)
                    nc.tensor.matmul(b_ps[:, js], ct_sb[:, jt, rs], ident[:], start=False, stop=True, is_transpose=True)
                b_sb = keep.tile([P, NP], F32, name="b_sb%d" % s, align_bytes=64,
                                 tag="b_last" if s == SLICES - 1 else "b_sb%d" % s)
                nc.scalar.copy(b_sb[:], b_ps[:])
                b_of[s] = b_sb

        def place(s):
            nc.vector.tensor_tensor(pages[PAGE_OF[s]][:].indirect(pos_sb[:]), b_of[s][:], wgs_sb[:], ALU.mult)

        zt = {}

        a_of = {}

        def frames(s, h):
            q, c0 = divmod(P * s, WA_COLS)
            cols = slice(HALF * h, HALF * (h + 1))
            a_ps = psum.tile([P, HALF], F32, name="a_ps", tag="a")
            for a in range(2):
                w0 = WA_COLS * a + c0
                nc.tensor.matmul_mx(
                    out=a_ps[:],
                    lhsT=wa_codes[q][:, w0:w0 + P].bitcast(FP8X4), lhsT_scale=wa_scales[q][:, w0:w0 + P],
                    rhs=vw[a][:, cols].bitcast(FP8X4), rhs_scale=vs[4 * (a + 1):P, cols],
                    start=(a == 0), stop=(a == 1))
            a_sb = work.tile([P, HALF], F32, name="a_sb", tag="a_sb", bufs=6)
            nc.vector.tensor_tensor(a_sb[:], a_ps[:], sit_sb[s][:, cols], ALU.mult)
            a_of[s, h] = a_sb

        def summed_transposes(s, c0, width, t_sb):
            h, a0 = divmod(c0, HALF)
            nc.vector.scalar_tensor_tensor(
                t_sb, a_of[s, h][:, a0:a0 + width], gz_sb[:, s:s + 1], pages[PAGE_OF[s]][:, c0:c0 + width],
                ALU.add, ALU.mult)
            zt_ps = psum.tile([P, width // P, P], F32, name="zt_ps", tag="tr")
            for jt in range(width // P):
                nc.tensor.matmul(zt_ps[:, jt, :], t_sb[:, P * jt:P * (jt + 1)], ident[:],
                                 start=True, stop=False, is_transpose=True)
                nc.tensor.matmul(zt_ps[:, jt, :], a_of[s, h][:, a0 + P * jt:a0 + P * (jt + 1)], ident[:],
                                 start=False, stop=True, is_transpose=True)
            return zt_ps

        def round_out(s, quarter, src):
            b, ss = divmod(s, 4)
            if ss == 0:
                zt[b, quarter] = work.tile([P, 2, 2, 2 * P], BF16, name="zt_sb", bufs=6)
            nc.scalar.copy(
                zt[b, quarter][:, :, :, 64 * ss:64 * (ss + 1)].rearrange("p u jt (m e) -> p u jt m e", e=2),
                src.rearrange("p jt (m u e) -> p u jt m e", u=2, e=2))

        def combine(s, h):
            zt_ps = summed_transposes(s, HALF * h, HALF, sit_sb[s + 1][:, HALF * h:HALF * (h + 1)])
            for q in range(2):
                round_out(s, 2 * h + q, zt_ps[:, 2 * q:2 * q + 2, :])

        def combine_last(quarter):
            t_sb = work.tile([P, QUARTER], F32, name="t_sb", tag="t_sb", bufs=4)
            zt_ps = summed_transposes(SLICES - 1, QUARTER * quarter, QUARTER, t_sb[:])
            round_out(SLICES - 1, quarter, zt_ps[:])

        def turn_words(b, quarter, zi_words, copy, tag):
            words = zt[b, quarter][:].rearrange("p u jt c -> p (u jt c)").bitcast(F32)
            w_ps = psum.tile([P, 2, 2, P], F32, name="w_ps", tag=tag, bufs=BANKS[tag])
            for jj in range(2):
                for u in range(2):
                    w0 = P * (2 * u + jj)
                    nc.tensor.transpose(w_ps[:, jj, u, :], words[:, w0:w0 + P], ident[:])
            copy(zi_words.rearrange("p (jj j u) -> p jj j u", jj=2, u=2), w_ps[:].rearrange("p jj u j -> p jj j u"))

        zi_of = {}

        def turn_first(h):
            zi = work.tile([P, 4 * HALF], BF16, name="zi", align_bytes=64)
            zi_of[h] = zi
            for q in range(2):
                turn_words(0, 2 * h + q, zi[:].bitcast(F32)[:, HALF * q:HALF * (q + 1)], nc.scalar.copy, "tr")

        def quantise_first(h):
            nc.vector.quantize_mx(out=z_codes[0][h][:].bitcast(FP8X4), scales=z_scales[0][h][:], in_=zi_of[h][:])

        def quantise_second(quarter):
            h, q = divmod(quarter, 2)
            cols = slice(QUARTER * q, QUARTER * (q + 1))
            ziq = work.tile([P, 4 * QUARTER], BF16, name="ziq", tag="big", bufs=3, align_bytes=64)
            turn_words(1, quarter, ziq[:].bitcast(F32), nc.vector.tensor_copy, "co")
            nc.vector.quantize_mx(out=z_codes[1][h][:, cols].bitcast(FP8X4), scales=z_scales[1][h][:, cols], in_=ziq[:])

        y_of = {}

        def open_sum(h, nt, tag):
            y_ps = psum.tile([P, HALF], F32, name="y_ps", tag=tag, bufs=BANKS[tag])
            y_of[h, nt] = y_ps
            nc.tensor.matmul_mx(
                out=y_ps[:],
                lhsT=wo_codes[0][:, P * nt:P * (nt + 1)].bitcast(FP8X4), lhsT_scale=wo_scales[0][:, P * nt:P * (nt + 1)],
                rhs=z_codes[0][h][:].bitcast(FP8X4), rhs_scale=z_scales[0][h][:],
                start=True, stop=False)

        def add_second(quarter):
            h, q = divmod(quarter, 2)
            cols = slice(QUARTER * q, QUARTER * (q + 1))
            for nt in range(N // P):
                w0 = P * nt
                nc.tensor.matmul_mx(
                    out=y_of[h, nt][:, cols],
                    lhsT=wo_codes[1][:, w0:w0 + P].bitcast(FP8X4), lhsT_scale=wo_scales[1][:, w0:w0 + P],
                    rhs=z_codes[1][h][:, cols].bitcast(FP8X4), rhs_scale=z_scales[1][h][:, cols],
                    start=False, stop=(q == 1))

        def read_out(h):
            for nt in range(N // P):
                o_sb = work.tile([P, HALF], F32, name="o_sb", tag="sit", bufs=6)
                nc.scalar.activation(o_sb[:], y_of[h, nt][:], ACT.Sigmoid)
                nc.sync.dma_start(out[P * nt:P * (nt + 1), HALF * h:HALF * (h + 1)], o_sb[:])

        def finish(quarter):
            quantise_second(quarter)
            if quarter == 2:
                for nt in range(N // P):
                    open_sum(1, nt, "a")
            add_second(quarter)
            if quarter % 2 == 1:
                read_out(quarter // 2)

        load_wa(0)
        load_words(tw[0], tab_words[0])
        move_planes(0)
        load_words(tw[1], tab_words[1])
        move_planes(1)
        load_wa(1)
        load_sit(0)
        load_sit(1)
        load_wa(2)
        load_sit(2)
        load_sit(3)
        load_wa(3)
        load_sit(4)
        load_sit(5)

        for s in range(DIRECT):
            measure_direct(s, "co")
        measure_turned()
        load_wo()
        load_sit(6)
        load_sit(7)
        place(0)
        place(1)
        nc.vector.tensor_copy(vw[0][:], tw[0][:].bitcast(U32).indirect(offs_sb[:]))
        place(2)
        quantise_wa(0)
        for h in range(2):
            nc.vector.tensor_copy(
                vw[1][:, HALF * h:HALF * (h + 1)], tw[1][:].bitcast(U32).indirect(offs_sb[:, 32 * h:32 * (h + 1)]))
        frames(0, 0)
        frames(0, 1)
        next_on_page = {1:[3],3:[4],4:[5],5:[6],6:[7]}
        for s in range(SLICES - 1):
            if s in (0, 2, 4):
                quantise_wa(s // 2 + 1)
            if s == 5:
                round_wo()
                quantise_wo(0)
            frames(s + 1, 0)
            frames(s + 1, 1)
            combine(s, 0)
            combine(s, 1)
            for k in next_on_page.get(s, ()):
                place(k)
            if s == 3:
                turn_first(0)
                quantise_first(0)
                turn_first(1)
        for nt in range(3):
            open_sum(0, nt, "a")
        combine_last(0)
        combine_last(1)
        quantise_wo(1)
        finish(0)
        combine_last(2)
        finish(1)
        combine_last(3)
        quantise_first(1)
        finish(2)
        finish(3)
